import numpy as np
import ml_dtypes


def mxq(x, axis, fmt="e4m3"):
    dtype, down = {"e4m3": (ml_dtypes.float8_e4m3fn, 7), "e5m2": (ml_dtypes.float8_e5m2, 14)}[fmt]
    v = np.moveaxis(np.asarray(x, np.float32).astype(ml_dtypes.bfloat16).astype(np.float64), axis, -1)
    blocks = v.reshape(v.shape[:-1] + (-1, 32))
    amax = np.abs(blocks).max(-1, keepdims=True)
    byte = np.maximum(np.where(amax > 0, np.frexp(amax)[1] - 1 + 127, 0) - down, 1)
    scale = np.exp2(byte - 127.0)
    codes = (blocks / scale).astype(np.float32).astype(dtype).astype(np.float64)
    return np.moveaxis((codes * scale).reshape(v.shape), -1, axis)


WIDE = False


def mx_kscale(k):
    if not WIDE:
        return np.ones(k)
    levels = np.array([10, -10, 5, -5, 0])
    if k % 512:
        return np.exp2(np.random.permutation(np.resize(levels, k // 32))).repeat(32)
    a = np.empty((k // 512, 16))
    for p in range(k // 512):
        a[p, :8] = np.random.permutation(np.resize(levels, 8))
        for g in range(8):
            far = levels[np.abs(levels - a[p, g]) >= 10]
            a[p, g + 8] = far[np.random.randint(len(far))]
    return np.exp2(a.ravel()).repeat(32)


def f64(x):
    return np.asarray(x).astype(np.float64)


def striped(idx):
    return np.tile(idx.reshape(-1, 16).T, (8, 1)).astype(np.uint16)


def unstriped(offs):
    return offs[:16].T.reshape(-1).astype(np.int64)


def striped8(idx):
    return np.concatenate([x.reshape(-1, 16).T for x in idx]).astype(np.uint16)


def runs(offs, k):
    lists = np.stack([offs[16 * r : 16 * r + 16].T.reshape(-1) for r in range(8)]).astype(np.int64)
    return lists[np.arange(k) % 512 // 64]


def pack_weight(w):
    k, n = w.shape
    w = f64(np.asarray(w, np.float32).astype(ml_dtypes.bfloat16)).reshape(k // 32, 32, n)
    amax = np.abs(w).max(1)
    byte = np.clip(np.where(amax > 0, np.frexp(amax)[1] - 1 + 127 - 7, 1), 1, 254)
    scaled = (w * np.exp2(127.0 - byte)[:, None, :]).reshape(k, n).astype(np.float32)
    words = np.ascontiguousarray(scaled.reshape(k // 512, 128, 4, n).transpose(0, 1, 3, 2)).astype(ml_dtypes.float8_e4m3fn).view(np.uint8)
    return words, np.ascontiguousarray(byte.astype(np.uint8).reshape(k // 512, 16, n))


def unpack_weight(words, scales):
    g, p, n, _ = words.shape
    vals = np.ascontiguousarray(words).view(ml_dtypes.float8_e4m3fn).astype(np.float64) * np.repeat(np.exp2(scales.astype(np.float64) - 127.0), 8, axis=1)[..., None]
    return vals.transpose(0, 1, 3, 2).reshape(g * 512, n)


K, T, S, N, H = 512, 2048, 512, 512, 512


def setup_inputs():
    n = np.random.standard_normal
    s = mx_kscale(K)[:, None]
    u = mx_kscale(H)
    packed_xT = pack_weight(n((K, T)) * s)
    return {
        "x_words": packed_xT[0],
        "x_scales": packed_xT[1],
        "w1": (n((K, H)) / np.sqrt(K) / s).astype(np.float32),
        "gn": (np.random.uniform(0.5, 1.5, (H, 1)) * u[:, None]).astype(np.float32),
        "w2": (n((H, N)) / np.sqrt(H) / u[:, None]).astype(np.float32),
        "offs": striped(np.random.permutation(T)[:S]),
        "n1": striped8(np.stack([np.random.permutation(S) for _ in range(8)])),
        "n2": striped8(np.stack([np.random.permutation(S) for _ in range(8)])),
        "n3": striped8(np.stack([np.random.permutation(S) for _ in range(8)])),
        "n4": striped8(np.stack([np.random.permutation(S) for _ in range(8)])),
    }


def reference(x_words, x_scales, w1, gn, w2, offs, n1, n2, n3, n4):
    xq = unpack_weight(x_words, x_scales)[:, unstriped(offs)]
    y = mxq(f64(w1), 0, "e4m3").T @ xq
    st = y + 0.5 * (y[np.arange(H)[:, None], runs(n1, H)])
    z = f64(gn) * (st - (st[np.arange(H)[:, None], runs(n2, H)]))
    h = mxq(f64(w2), 0, "e4m3").T @ mxq(z, 0, "e4m3")
    return h * (h[np.arange(N)[:, None], runs(n3, N)] - (h[np.arange(N)[:, None], runs(n4, N)]))

@@ -1,0 +1,220 @@
+from contextlib import ExitStack
+
+import concourse.mybir as mybir
+
+K, T, S, H, N = 512, 2048, 512, 512, 512
+FLOPS = 2 * K * H * S + 2 * H * N * S
+
+F32 = mybir.dt.float32
+BF16 = mybir.dt.bfloat16
+I32 = mybir.dt.int32
+U32 = mybir.dt.uint32
+U16 = mybir.dt.uint16
+U8 = mybir.dt.uint8
+FP8X4 = mybir.dt.float8_e4m3fn_x4
+ADD = mybir.AluOpType.add
+SUB = mybir.AluOpType.subtract
+MULT = mybir.AluOpType.mult
+COPY = mybir.ActivationFunctionType.Copy
+
+P = 128
+PACK = 4
+HALF = S // 2
+Z_PIECES = ((0, 256), (256, 384), (384, 512))
+
+
+def cols16(a, b):
+    return slice(a // 16, b // 16)
+
+
+def tile_picked_layhopwind_none_p_kernel(tc, x_words, x_scales, w1, gn, w2, offs, n1, n2, n3, n4, out):
+    nc = tc.nc
+    with ExitStack() as ctx:
+        keep = ctx.enter_context(tc.tile_pool(name="keep", bufs=1))
+        psum = ctx.enter_context(tc.psum_pool(name="psum", bufs=1))
+
+        def sb(name, shape, dtype):
+            return keep.tile(shape, dtype, name=name, align_bytes=64)
+
+        lists = {}
+        for name in ("offs", "n1", "n2", "n3", "n4"):
+            lists[name] = sb("list_" + name, [P, S // 16], U16)
+
+        x_bytes = sb("x_bytes", [P, T], U8)
+        nc.vector.memset(x_bytes[:].bitcast(I32), 0)
+        gain = sb("gain", [P, PACK], F32)
+        nc.sync.dma_start(out=gain[:], in_=gn.rearrange("(p t) o -> p (t o)", t=PACK))
+        nc.sync.dma_start(lists["offs"][:], offs)
+        for q in range(4):
+            nc.scalar.dma_start(out=x_bytes[32 * q : 32 * q + 4, :].bitcast(I32), in_=x_scales[0, 4 * q : 4 * q + 4, :].bitcast(I32))
+        w1_rows = w1.rearrange("(p j) c -> p j c", j=PACK)
+        w1_raw = []
+        for u in range(2):
+            raw = sb("w1_raw%d" % u, [P, PACK, H // 2], F32)
+            nc.sync.dma_start(out=raw[:], in_=w1_rows[:, :, u * (H // 2) : (u + 1) * (H // 2)])
+            w1_raw.append(raw)
+        x_table = sb("x_table", [P, T], I32)
+        nc.sync.dma_start(out=x_table[:], in_=x_words[0].rearrange("p n r -> p (n r)").bitcast(I32))
+        nc.sync.dma_start(lists["n1"][:], n1)
+        nc.sync.dma_start(lists["n2"][:], n2)
+        w2_raw = sb("w2_raw", [P, PACK, N], F32)
+        nc.sync.dma_start(out=w2_raw[:], in_=w2.rearrange("(p j) c -> p j c", j=PACK))
+        nc.sync.dma_start(lists["n3"][:], n3)
+        nc.sync.dma_start(lists["n4"][:], n4)
+
+        gain_full = sb("gain_full", [P, PACK], F32)
+        gain_half = sb("gain_half", [P, PACK], F32)
+        nc.scalar.activation(gain_full[:], gain[:], COPY, scale=-1.0)
+        nc.scalar.activation(gain_half[:], gain[:], COPY, scale=-0.5)
+
+        xq_scales = sb("xq_scales", [P, S], U8)
+        nc.vector.tensor_copy(xq_scales[:], x_bytes[:].indirect(lists["offs"][:]))
+
+        w1_b = sb("w1_b", [P, PACK, P, PACK], BF16)
+        w1_dst = w1_b[:].rearrange("p t m j -> p m j t")
+        src0 = w1_raw[0][:].rearrange("p j (m t) -> p m j t", t=PACK)
+        src1 = w1_raw[1][:].rearrange("p j (m t) -> p m j t", t=PACK)
+        nc.scalar.copy(w1_dst[:, 0:32], src0[:, 0:32])
+        nc.vector.tensor_copy(w1_dst[:, 32:64], src0[:, 32:64])
+        nc.scalar.copy(w1_dst[:, 64:80], src1[:, 0:16])
+        nc.vector.tensor_copy(w1_dst[:, 80:128], src1[:, 16:64])
+        w1_codes = sb("w1_codes", [P, H], U32)
+        w1_scales = sb("w1_scales", [P, H], U8)
+        nc.vector.quantize_mx(out=w1_codes[:].bitcast(FP8X4), scales=w1_scales[:], in_=w1_b[:].rearrange("p t m j -> p (t m j)"))
+
+        xq_words = sb("xq_words", [P, S], U32)
+        for u in range(2):
+            a, b = u * HALF, (u + 1) * HALF
+            nc.vector.tensor_copy(xq_words[:, a:b], x_table[:].bitcast(U32).indirect(lists["offs"][:, cols16(a, b)]))
+
+        banks = [psum.tile([P, S], F32, name="bank%d" % i) for i in range(8)]
+
+        def mm(dst, codes, scales, t, rhs, rhs_scales):
+            nc.tensor.matmul_mx(out=dst, lhsT=codes[:, t * P : (t + 1) * P].bitcast(FP8X4), lhsT_scale=scales[:, t * P : (t + 1) * P],
+                                rhs=rhs.bitcast(FP8X4), rhs_scale=rhs_scales, start=True, stop=True)
+
+        half_win = [sb("half_win0", [P, S], F32)] + [sb("half_win%d" % t, [P, 2 * S], F32) for t in range(1, PACK)]
+        y_last = sb("y_last", [P, S], F32)
+        y_full = [half_win[t + 1][:, S:] for t in range(PACK - 1)] + [y_last[:]]
+        st_win = [sb("st_win%d" % t, [P, S], F32) for t in range(PACK)]
+        h_win = [sb("h_win%d" % t, [P, 2 * S], F32) for t in range(PACK)]
+        st_copy = [h_win[t][:, S:] for t in range(PACK)]
+
+        for u in range(2):
+            a, b = u * HALF, (u + 1) * HALF
+            bank = banks[4 * u]
+            mm(bank[:, 0:HALF], w1_codes, w1_scales, 0, xq_words[:, a:b], xq_scales[:, a:b])
+            nc.scalar.activation(half_win[0][:, a:b], bank[:, 0:HALF], COPY, scale=gain_half[:, 0:1])
+            nc.scalar.activation(y_full[0][:, a:b], bank[:, 0:HALF], COPY, scale=gain_full[:, 0:1])
+        for t in range(1, PACK):
+            mm(banks[t][:], w1_codes, w1_scales, t, xq_words[:], xq_scales[:])
+        for u in range(2):
+            a, b = u * HALF, (u + 1) * HALF
+            nc.vector.tensor_tensor(st_win[0][:, a:b], half_win[0][:].indirect(lists["n1"][:, cols16(a, b)]), y_full[0][:, a:b], ADD)
+        for t in range(1, PACK):
+            nc.scalar.activation(half_win[t][:, 0:S], banks[t][:], COPY, scale=gain_half[:, t : t + 1])
+            nc.scalar.activation(y_full[t], banks[t][:], COPY, scale=gain_full[:, t : t + 1])
+            nc.vector.tensor_tensor(st_win[t][:], half_win[t][:].indirect(lists["n1"][:]), y_full[t], ADD)
+        for t in range(PACK):
+            nc.scalar.copy(st_copy[t], st_win[t][:])
+
+        w2_b = sb("w2_b", [P, PACK, P, PACK], BF16)
+        w2_codes = sb("w2_codes", [P, N], U32)
+        w2_scales = sb("w2_scales", [P, N], U8)
+        w2_src = w2_raw[:].rearrange("p j (q t r i) -> p t q r j i", t=PACK, r=2, i=4)
+
+        def w2_weave(t, copy):
+            copy(w2_b[:, t].rearrange("p (q r i) j -> p q r j i", r=2, i=4), w2_src[:, t])
+
+        def w2_quant(t0, t1):
+            nc.vector.quantize_mx(out=w2_codes[:, t0 * P : t1 * P].bitcast(FP8X4), scales=w2_scales[:, t0 * P : t1 * P],
+                                  in_=w2_b[:, t0:t1].rearrange("p t m j -> p (t m j)"))
+
+        w2_weave(0, nc.scalar.copy)
+        w2_weave(1, nc.scalar.copy)
+
+        z_codes = sb("z_codes", [P, S], U32)
+        z_scales = sb("z_scales", [P, S], U8)
+        last = len(Z_PIECES) - 1
+        z32 = []
+        z_b = []
+        for i, (a, b) in enumerate(Z_PIECES):
+            z32.append(sb("z32_%d" % i, [P, PACK, b - a], F32))
+            z_b.append(sb("z_b%d" % i, [P, b - a, PACK], BF16))
+
+        def z_gather(i):
+            a, b = Z_PIECES[i]
+            for t in range(PACK):
+                nc.vector.tensor_tensor(z32[i][:, t, :], st_win[t][:].indirect(lists["n2"][:, cols16(a, b)]), st_copy[t][:, a:b], SUB)
+
+        def z_weave(i, copy):
+            copy(z_b[i][:].rearrange("p (c i) t -> p c t i", i=4), z32[i][:].rearrange("p t (c i) -> p c t i", i=4))
+
+        def z_quant(i):
+            a, b = Z_PIECES[i]
+            nc.vector.quantize_mx(out=z_codes[:, a:b].bitcast(FP8X4), scales=z_scales[:, a:b], in_=z_b[i][:].rearrange("p s t -> p (s t)"))
+
+        def h_bank(t, i):
+            return banks[0] if (t == 0 and i == last) else banks[4 + t]
+
+        def h_mm(t, i):
+            a, b = Z_PIECES[i]
+            mm(h_bank(t, i)[:, a:b], w2_codes, w2_scales, t, z_codes[:, a:b], z_scales[:, a:b])
+
+        z_gather(0)
+        z_weave(0, nc.scalar.copy)
+        w2_quant(0, 2)
+        z_gather(1)
+        z_weave(1, nc.scalar.copy)
+        z_gather(2)
+        z_quant(0)
+        z_weave(2, nc.vector.tensor_copy)
+        z_quant(1)
+        w2_weave(2, nc.vector.tensor_copy)
+        z_quant(2)
+        w2_weave(3, nc.vector.tensor_copy)
+        w2_quant(2, 3)
+        w2_quant(3, 4)
+        h_mm(0, 0)
+        h_mm(0, 1)
+        split = Z_PIECES[last][0]
+        nc.scalar.copy(h_win[0][:, 0:split], banks[4][:, 0:split])
+        h_mm(1, 0)
+        h_mm(1, 1)
+        h_mm(0, 2)
+        nc.scalar.copy(h_win[0][:, split:S], banks[0][:, split:S])
+        h_mm(1, 2)
+        nc.scalar.copy(h_win[1][:, 0:S], banks[5][:])
+        for t in range(2, PACK):
+            mm(banks[4 + t][:], w2_codes, w2_scales, t, z_codes[:], z_scales[:])
+            nc.scalar.copy(h_win[t][:, 0:S], banks[4 + t][:])
+
+        out_rows = out.rearrange("(q t r) s -> t q r s", t=PACK, r=8)
+        far = [sb("far%d" % t, [P, S], F32) for t in range(PACK)]
+        diff = [sb("diff%d" % t, [P, S], F32) for t in range(PACK)]
+        res = [sb("res%d" % t, [P, S], F32) for t in range(PACK)]
+
+        def g4(t):
+            nc.vector.tensor_copy(far[t][:], h_win[t][:].indirect(lists["n4"][:]))
+
+        def d3(t, a, b):
+            nc.vector.tensor_tensor(diff[t][:, a:b], h_win[t][:].indirect(lists["n3"][:, cols16(a, b)]), far[t][:, a:b], SUB)
+
+        def fin(t, a, b):
+            nc.vector.tensor_tensor(res[t][:, a:b], diff[t][:, a:b], h_win[t][:, a:b], MULT)
+            nc.sync.dma_start(out=out_rows[t][:, :, a:b], in_=res[t][:, a:b])
+
+        g4(0)
+        g4(1)
+        d3(0, 0, S)
+        g4(2)
+        fin(0, 0, S)
+        d3(1, 0, S)
+        g4(3)
+        fin(1, 0, S)
+        d3(2, 0, S)
+        d3(3, 0, HALF)
+        fin(2, 0, S)
+        d3(3, HALF, S)
+        fin(3, 0, HALF)
+        fin(3, HALF, S)

@@ -33,8 +33,8 @@ def tile_picked_layhopwind_none_p_kernel(tc, x_words, x_scales, w1, gn, w2, offs
         keep = ctx.enter_context(tc.tile_pool(name="keep", bufs=1))
         psum = ctx.enter_context(tc.psum_pool(name="psum", bufs=1))
 
-        def sb(name, shape, dtype):
-            return keep.tile(shape, dtype, name=name, align_bytes=64)
+        def sb(name, shape, dtype, tag=""):
+            return keep.tile(shape, dtype, name=name, tag=tag or name, align_bytes=64)
 
         lists = {}
         for name in ("offs", "n1", "n2", "n3", "n4"):
@@ -42,19 +42,17 @@ def tile_picked_layhopwind_none_p_kernel(tc, x_words, x_scales, w1, gn, w2, offs
 
         x_bytes = sb("x_bytes", [P, T], U8)
         nc.vector.memset(x_bytes[:].bitcast(I32), 0)
-        gain = sb("gain", [P, PACK], F32)
-        nc.sync.dma_start(out=gain[:], in_=gn.rearrange("(p t) o -> p (t o)", t=PACK))
-        nc.sync.dma_start(lists["offs"][:], offs)
-        for q in range(4):
-            nc.scalar.dma_start(out=x_bytes[32 * q : 32 * q + 4, :].bitcast(I32), in_=x_scales[0, 4 * q : 4 * q + 4, :].bitcast(I32))
         w1_rows = w1.rearrange("(p j) c -> p j c", j=PACK)
-        w1_raw = []
-        for u in range(2):
-            raw = sb("w1_raw%d" % u, [P, PACK, H // 2], F32)
-            nc.sync.dma_start(out=raw[:], in_=w1_rows[:, :, u * (H // 2) : (u + 1) * (H // 2)])
-            w1_raw.append(raw)
+        w1_raw = [sb("w1_raw%d" % u, [P, PACK, H // 2], F32) for u in range(2)]
+        nc.sync.dma_start(out=w1_raw[0][:], in_=w1_rows[:, :, 0 : H // 2])
+        for q in range(4):
+            nc.sync.dma_start(out=x_bytes[32 * q : 32 * q + 4, :].bitcast(I32), in_=x_scales[0, 4 * q : 4 * q + 4, :].bitcast(I32))
+        nc.sync.dma_start(lists["offs"][:], offs)
+        nc.sync.dma_start(out=w1_raw[1][:], in_=w1_rows[:, :, H // 2 : H])
         x_table = sb("x_table", [P, T], I32)
         nc.sync.dma_start(out=x_table[:], in_=x_words[0].rearrange("p n r -> p (n r)").bitcast(I32))
+        gain = sb("gain", [P, PACK], F32)
+        nc.gpsimd.dma_start(out=gain[:], in_=gn.rearrange("(p t) o -> p (t o)", t=PACK))
         nc.sync.dma_start(lists["n1"][:], n1)
         nc.sync.dma_start(lists["n2"][:], n2)
         w2_raw = sb("w2_raw", [P, PACK, N], F32)
@@ -64,23 +62,25 @@ def tile_picked_layhopwind_none_p_kernel(tc, x_words, x_scales, w1, gn, w2, offs
 
         gain_full = sb("gain_full", [P, PACK], F32)
         gain_half = sb("gain_half", [P, PACK], F32)
-        nc.scalar.activation(gain_full[:], gain[:], COPY, scale=-1.0)
-        nc.scalar.activation(gain_half[:], gain[:], COPY, scale=-0.5)
+        nc.gpsimd.tensor_scalar(gain_half[:], gain[:], -0.5, 0.0, MULT, ADD)
+        nc.gpsimd.tensor_scalar(gain_full[:], gain[:], -1.0, 0.0, MULT, ADD)
 
         xq_scales = sb("xq_scales", [P, S], U8)
         nc.vector.tensor_copy(xq_scales[:], x_bytes[:].indirect(lists["offs"][:]))
 
         w1_b = sb("w1_b", [P, PACK, P, PACK], BF16)
-        w1_dst = w1_b[:].rearrange("p t m j -> p m j t")
-        src0 = w1_raw[0][:].rearrange("p j (m t) -> p m j t", t=PACK)
-        src1 = w1_raw[1][:].rearrange("p j (m t) -> p m j t", t=PACK)
-        nc.scalar.copy(w1_dst[:, 0:32], src0[:, 0:32])
-        nc.vector.tensor_copy(w1_dst[:, 32:64], src0[:, 32:64])
-        nc.scalar.copy(w1_dst[:, 64:80], src1[:, 0:16])
-        nc.vector.tensor_copy(w1_dst[:, 80:128], src1[:, 16:64])
+        w1_dst = w1_b[:].rearrange("p (a b) m j -> p a m j b", b=2)
+        for u in range(2):
+            src = w1_raw[u][:].rearrange("p j (m a b) -> p a m j b", a=2, b=2)
+            m0 = u * 64
+            nc.vector.tensor_copy(w1_dst[:, 0, m0 : m0 + 64], src[:, 0])
+            nc.scalar.copy(w1_dst[:, 1, m0 : m0 + 40], src[:, 1, 0:40])
+            nc.vector.tensor_copy(w1_dst[:, 1, m0 + 40 : m0 + 64], src[:, 1, 40:64])
         w1_codes = sb("w1_codes", [P, H], U32)
         w1_scales = sb("w1_scales", [P, H], U8)
-        nc.vector.quantize_mx(out=w1_codes[:].bitcast(FP8X4), scales=w1_scales[:], in_=w1_b[:].rearrange("p t m j -> p (t m j)"))
+        for a in range(2):
+            nc.vector.quantize_mx(out=w1_codes[:, a * 256 : (a + 1) * 256].bitcast(FP8X4), scales=w1_scales[:, a * 256 : (a + 1) * 256],
+                                  in_=w1_b[:, 2 * a : 2 * a + 2].rearrange("p t m j -> p (t m j)"))
 
         xq_words = sb("xq_words", [P, S], U32)
         for u in range(2):
@@ -97,15 +97,19 @@ def tile_picked_layhopwind_none_p_kernel(tc, x_words, x_scales, w1, gn, w2, offs
         y_last = sb("y_last", [P, S], F32)
         y_full = [half_win[t + 1][:, S:] for t in range(PACK - 1)] + [y_last[:]]
         st_win = [sb("st_win%d" % t, [P, S], F32) for t in range(PACK)]
-        h_win = [sb("h_win%d" % t, [P, 2 * S], F32) for t in range(PACK)]
-        st_copy = [h_win[t][:, S:] for t in range(PACK)]
+        h_win = [sb("h_win%d" % t, [P, 2 * S], F32) for t in range(PACK - 1)] + [sb("h_win3", [P, S], F32)]
+        st_last = sb("st_last", [P, S], F32)
+        st_copy = [h_win[t][:, S:] for t in range(PACK - 1)] + [st_last[:]]
 
         for u in range(2):
             a, b = u * HALF, (u + 1) * HALF
             bank = banks[4 * u]
             mm(bank[:, 0:HALF], w1_codes, w1_scales, 0, xq_words[:, a:b], xq_scales[:, a:b])
             nc.scalar.activation(half_win[0][:, a:b], bank[:, 0:HALF], COPY, scale=gain_half[:, 0:1])
-            nc.scalar.activation(y_full[0][:, a:b], bank[:, 0:HALF], COPY, scale=gain_full[:, 0:1])
+            if u == 0:
+                nc.vector.tensor_scalar(y_full[0][:, a:b], bank[:, 0:HALF], gain_full[:, 0:1], None, MULT)
+            else:
+                nc.scalar.activation(y_full[0][:, a:b], bank[:, 0:HALF], COPY, scale=gain_full[:, 0:1])
         for t in range(1, PACK):
             mm(banks[t][:], w1_codes, w1_scales, t, xq_words[:], xq_scales[:])
         for u in range(2):
@@ -116,22 +120,28 @@ def tile_picked_layhopwind_none_p_kernel(tc, x_words, x_scales, w1, gn, w2, offs
             nc.scalar.activation(y_full[t], banks[t][:], COPY, scale=gain_full[:, t : t + 1])
             nc.vector.tensor_tensor(st_win[t][:], half_win[t][:].indirect(lists["n1"][:]), y_full[t], ADD)
         for t in range(PACK):
-            nc.scalar.copy(st_copy[t], st_win[t][:])
+            if t < 2:
+                nc.sync.dma_start(out=st_copy[t], in_=st_win[t][:])
+            else:
+                nc.scalar.copy(st_copy[t], st_win[t][:])
 
-        w2_b = sb("w2_b", [P, PACK, P, PACK], BF16)
         w2_codes = sb("w2_codes", [P, N], U32)
         w2_scales = sb("w2_scales", [P, N], U8)
         w2_src = w2_raw[:].rearrange("p j (q t r i) -> p t q r j i", t=PACK, r=2, i=4)
 
-        def w2_weave(t, copy):
-            copy(w2_b[:, t].rearrange("p (q r i) j -> p q r j i", r=2, i=4), w2_src[:, t])
+        def w2_weave(dst, t, copy):
+            copy(dst.rearrange("p (q r i) j -> p q r j i", r=2, i=4), w2_src[:, t])
 
-        def w2_quant(t0, t1):
+        def w2_quant(src, t0, t1):
             nc.vector.quantize_mx(out=w2_codes[:, t0 * P : t1 * P].bitcast(FP8X4), scales=w2_scales[:, t0 * P : t1 * P],
-                                  in_=w2_b[:, t0:t1].rearrange("p t m j -> p (t m j)"))
+                                  in_=src.rearrange("p t m j -> p (t m j)"))
 
-        w2_weave(0, nc.scalar.copy)
-        w2_weave(1, nc.scalar.copy)
+        w2_early = sb("w2_early", [P, 2, P, PACK], BF16)
+        w2_late = sb("w2_late", [P, 2, P, PACK], BF16)
+        w2_weave(w2_early[:, 0], 0, nc.scalar.copy)
+        w2_weave(w2_early[:, 1], 1, nc.scalar.copy)
+        w2_weave(w2_late[:, 0], 2, nc.scalar.copy)
+        w2_weave(w2_late[:, 1], 3, nc.scalar.copy)
 
         z_codes = sb("z_codes", [P, S], U32)
         z_scales = sb("z_scales", [P, S], U8)
@@ -163,18 +173,15 @@ def tile_picked_layhopwind_none_p_kernel(tc, x_words, x_scales, w1, gn, w2, offs
 
         z_gather(0)
         z_weave(0, nc.scalar.copy)
-        w2_quant(0, 2)
         z_gather(1)
         z_weave(1, nc.scalar.copy)
         z_gather(2)
+        z_weave(2, nc.scalar.copy)
+        w2_quant(w2_early[:], 0, 2)
         z_quant(0)
-        z_weave(2, nc.vector.tensor_copy)
         z_quant(1)
-        w2_weave(2, nc.vector.tensor_copy)
         z_quant(2)
-        w2_weave(3, nc.vector.tensor_copy)
-        w2_quant(2, 3)
-        w2_quant(3, 4)
+        w2_quant(w2_late[:], 2, 4)
         h_mm(0, 0)
         h_mm(0, 1)
         split = Z_PIECES[last][0]
@@ -194,27 +201,32 @@ def tile_picked_layhopwind_none_p_kernel(tc, x_words, x_scales, w1, gn, w2, offs
         diff = [sb("diff%d" % t, [P, S], F32) for t in range(PACK)]
         res = [sb("res%d" % t, [P, S], F32) for t in range(PACK)]
 
-        def g4(t):
-            nc.vector.tensor_copy(far[t][:], h_win[t][:].indirect(lists["n4"][:]))
+        def g4(t, a, b):
+            nc.vector.tensor_copy(far[t][:, a:b], h_win[t][:].indirect(lists["n4"][:, cols16(a, b)]))
 
         def d3(t, a, b):
             nc.vector.tensor_tensor(diff[t][:, a:b], h_win[t][:].indirect(lists["n3"][:, cols16(a, b)]), far[t][:, a:b], SUB)
 
-        def fin(t, a, b):
-            nc.vector.tensor_tensor(res[t][:, a:b], diff[t][:, a:b], h_win[t][:, a:b], MULT)
+        def fin(t, a, b, eng):
+            eng.tensor_tensor(res[t][:, a:b], diff[t][:, a:b], h_win[t][:, a:b], MULT)
             nc.sync.dma_start(out=out_rows[t][:, :, a:b], in_=res[t][:, a:b])
 
-        g4(0)
-        g4(1)
-        d3(0, 0, S)
-        g4(2)
-        fin(0, 0, S)
+        g4(0, 0, HALF)
+        g4(0, HALF, S)
+        d3(0, 0, HALF)
+        d3(0, HALF, S)
+        g4(1, 0, S)
+        fin(0, 0, S, nc.vector)
+        g4(2, 0, S)
         d3(1, 0, S)
-        g4(3)
-        fin(1, 0, S)
+        g4(3, 0, HALF)
+        g4(3, HALF, S)
+        fin(1, 0, S, nc.vector)
         d3(2, 0, S)
         d3(3, 0, HALF)
-        fin(2, 0, S)
-        d3(3, HALF, S)
-        fin(3, 0, HALF)
-        fin(3, HALF, S)
+        fin(2, 0, S, nc.vector)
+        d3(3, HALF, 384)
+        fin(3, 0, HALF, nc.vector)
+        d3(3, 384, S)
+        fin(3, HALF, 384, nc.vector)
+        fin(3, 384, S, nc.vector)

@@ -46,7 +46,7 @@ def tile_picked_layhopwind_none_p_kernel(tc, x_words, x_scales, w1, gn, w2, offs
         w1_raw = [sb("w1_raw%d" % u, [P, PACK, H // 2], F32) for u in range(2)]
         nc.sync.dma_start(out=w1_raw[0][:], in_=w1_rows[:, :, 0 : H // 2])
         for q in range(4):
-            nc.sync.dma_start(out=x_bytes[32 * q : 32 * q + 4, :].bitcast(I32), in_=x_scales[0, 4 * q : 4 * q + 4, :].bitcast(I32))
+            nc.sync.dma_start(out=x_bytes[q:P:32, :].bitcast(I32), in_=x_scales[0, q:16:4, :].bitcast(I32))
         nc.sync.dma_start(lists["offs"][:], offs)
         nc.sync.dma_start(out=w1_raw[1][:], in_=w1_rows[:, :, H // 2 : H])
         x_table = sb("x_table", [P, T], I32)
@@ -211,20 +211,15 @@ def tile_picked_layhopwind_none_p_kernel(tc, x_words, x_scales, w1, gn, w2, offs
             eng.tensor_tensor(res[t][:, a:b], diff[t][:, a:b], h_win[t][:, a:b], MULT)
             nc.sync.dma_start(out=out_rows[t][:, :, a:b], in_=res[t][:, a:b])
 
-        g4(0, 0, HALF)
-        g4(0, HALF, S)
-        d3(0, 0, HALF)
-        d3(0, HALF, S)
-        g4(1, 0, S)
-        fin(0, 0, S, nc.vector)
-        g4(2, 0, S)
-        d3(1, 0, S)
+        for t in range(PACK - 1):
+            g4(t, 0, HALF)
+            g4(t, HALF, S)
+            d3(t, 0, HALF)
+            d3(t, HALF, S)
+            fin(t, 0, S, nc.gpsimd)
         g4(3, 0, HALF)
         g4(3, HALF, S)
-        fin(1, 0, S, nc.vector)
-        d3(2, 0, S)
         d3(3, 0, HALF)
-        fin(2, 0, S, nc.vector)
         d3(3, HALF, 384)
         fin(3, 0, HALF, nc.vector)
         d3(3, 384, S)

@@ -1,6 +1,7 @@
 from contextlib import ExitStack
 
 import concourse.mybir as mybir
+from concourse.masks import make_identity
 
 K, T, S, H, N = 512, 2048, 512, 512, 512
 FLOPS = 2 * K * H * S + 2 * H * N * S
@@ -64,6 +65,9 @@ def tile_picked_layhopwind_none_p_kernel(tc, x_words, x_scales, w1, gn, w2, offs
         gain_half = sb("gain_half", [P, PACK], F32)
         nc.gpsimd.tensor_scalar(gain_half[:], gain[:], -0.5, 0.0, MULT, ADD)
         nc.gpsimd.tensor_scalar(gain_full[:], gain[:], -1.0, 0.0, MULT, ADD)
+
+        ident = sb("ident", [P, P], F32)
+        make_identity(nc, ident[:])
 
         xq_scales = sb("xq_scales", [P, S], U8)
         nc.vector.tensor_copy(xq_scales[:], x_bytes[:].indirect(lists["offs"][:]))
@@ -186,42 +190,80 @@ def tile_picked_layhopwind_none_p_kernel(tc, x_words, x_scales, w1, gn, w2, offs
         h_mm(0, 1)
         split = Z_PIECES[last][0]
         nc.scalar.copy(h_win[0][:, 0:split], banks[4][:, 0:split])
+        h_mm(0, 2)
         h_mm(1, 0)
         h_mm(1, 1)
-        h_mm(0, 2)
-        nc.scalar.copy(h_win[0][:, split:S], banks[0][:, split:S])
+        nc.vector.tensor_copy(h_win[0][:, split:S], banks[0][:, split:S])
         h_mm(1, 2)
-        nc.scalar.copy(h_win[1][:, 0:S], banks[5][:])
         for t in range(2, PACK):
             mm(banks[4 + t][:], w2_codes, w2_scales, t, z_codes[:], z_scales[:])
+        width = {1: S, 2: HALF}
+        h_pos = {t: sb("h_pos%d" % t, [P, w], F32) for t, w in width.items()}
+        h_neg = {t: sb("h_neg%d" % t, [P, w], F32) for t, w in width.items()}
+        for t, w in width.items():
             nc.scalar.copy(h_win[t][:, 0:S], banks[4 + t][:])
+            nc.scalar.copy(h_pos[t][:], banks[4 + t][:, 0:w])
+            nc.scalar.activation(h_neg[t][:], banks[4 + t][:, 0:w], COPY, scale=-1.0)
+        nc.scalar.copy(h_win[3][:], banks[7][:])
 
         out_rows = out.rearrange("(q t r) s -> t q r s", t=PACK, r=8)
-        far = [sb("far%d" % t, [P, S], F32) for t in range(PACK)]
-        diff = [sb("diff%d" % t, [P, S], F32) for t in range(PACK)]
         res = [sb("res%d" % t, [P, S], F32) for t in range(PACK)]
+        far = sb("far", [P, S], F32)
+        nc.vector.tensor_copy(far[:], h_win[0][:].indirect(lists["n4"][:]))
 
-        def g4(t, a, b):
-            nc.vector.tensor_copy(far[t][:, a:b], h_win[t][:].indirect(lists["n4"][:, cols16(a, b)]))
+        plus = {t: sb("plus%d" % t, [P, w], F32) for t, w in width.items()}
+        minus = {t: sb("minus%d" % t, [P, w], F32) for t, w in width.items()}
+        turned = {t: sb("turned%d" % t, [P, w], F32) for t, w in width.items()}
 
-        def d3(t, a, b):
-            nc.vector.tensor_tensor(diff[t][:, a:b], h_win[t][:].indirect(lists["n3"][:, cols16(a, b)]), far[t][:, a:b], SUB)
+        def term(dst, t, name, other, first):
+            w = width[t]
+            nc.vector.tensor_tensor(dst[:], h_win[t][:].indirect(lists[name][:, cols16(0, w)]), other[:], MULT)
+            for c in range(0, w, P):
+                nc.tensor.matmul(banks[t][:, c : c + P], dst[:, c : c + P], ident[:], start=(first and c == 0), stop=(not first and c == w - P), is_transpose=True)
 
-        def fin(t, a, b, eng):
-            eng.tensor_tensor(res[t][:, a:b], diff[t][:, a:b], h_win[t][:, a:b], MULT)
+        def terms_plus(t):
+            term(plus[t], t, "n3", h_pos[t], True)
+
+        def terms_minus(t):
+            term(minus[t], t, "n4", h_neg[t], False)
+            nc.scalar.copy(turned[t][:], banks[t][:, 0 : width[t]])
+
+        def turn_back(t):
+            w = width[t]
+            for c in range(0, w, P):
+                nc.tensor.transpose(banks[4 + t][:, c : c + P], turned[t][:, c : c + P], ident[:])
+            nc.scalar.copy(res[t][:, 0:w], banks[4 + t][:, 0:w])
+            nc.sync.dma_start(out=out_rows[t][:, :, 0:w], in_=res[t][:, 0:w])
+
+        terms_plus(1)
+        terms_minus(1)
+        terms_plus(2)
+        terms_minus(2)
+        turn_back(1)
+        turn_back(2)
+
+        def d3(dst, t, a, b, other):
+            nc.vector.tensor_tensor(dst, h_win[t][:].indirect(lists["n3"][:, cols16(a, b)]), other, SUB)
+
+        def fin(src, t, a, b):
+            nc.vector.tensor_tensor(res[t][:, a:b], src, h_win[t][:, a:b], MULT)
             nc.sync.dma_start(out=out_rows[t][:, :, a:b], in_=res[t][:, a:b])
 
-        for t in range(PACK - 1):
-            g4(t, 0, HALF)
-            g4(t, HALF, S)
-            d3(t, 0, HALF)
-            d3(t, HALF, S)
-            fin(t, 0, S, nc.gpsimd)
-        g4(3, 0, HALF)
-        g4(3, HALF, S)
-        d3(3, 0, HALF)
-        d3(3, HALF, 384)
-        fin(3, 0, HALF, nc.vector)
-        d3(3, 384, S)
-        fin(3, HALF, 384, nc.vector)
-        fin(3, 384, S, nc.vector)
+        far2 = sb("far2", [P, HALF], F32)
+        far3 = sb("far3", [P, S], F32)
+        diff0 = h_neg[1]
+        diff2 = sb("diff2", [P, HALF], F32)
+        diff3 = sb("diff3", [P, S], F32)
+        d3(diff0[:], 0, 0, S, far[:])
+        nc.vector.tensor_copy(far2[:], h_win[2][:].indirect(lists["n4"][:, cols16(HALF, S)]))
+        fin(diff0[:], 0, 0, S)
+        d3(diff2[:], 2, HALF, S, far2[:])
+        nc.vector.tensor_copy(far3[:, 0:HALF], h_win[3][:].indirect(lists["n4"][:, cols16(0, HALF)]))
+        fin(diff2[:], 2, HALF, S)
+        nc.vector.tensor_copy(far3[:, HALF:S], h_win[3][:].indirect(lists["n4"][:, cols16(HALF, S)]))
+        d3(diff3[:, 0:HALF], 3, 0, HALF, far3[:, 0:HALF])
+        d3(diff3[:, HALF:384], 3, HALF, 384, far3[:, HALF:384])
+        fin(diff3[:, 0:HALF], 3, 0, HALF)
+        d3(diff3[:, 384:S], 3, 384, S, far3[:, 384:S])
+        fin(diff3[:, HALF:384], 3, HALF, 384)
+        fin(diff3[:, 384:S], 3, 384, S)

from contextlib import ExitStack

import concourse.mybir as mybir
from concourse.masks import make_identity

K, T, S, H, N = 512, 2048, 512, 512, 512
FLOPS = 2 * K * H * S + 2 * H * N * S

F32 = mybir.dt.float32
BF16 = mybir.dt.bfloat16
I32 = mybir.dt.int32
U32 = mybir.dt.uint32
U16 = mybir.dt.uint16
U8 = mybir.dt.uint8
FP8X4 = mybir.dt.float8_e4m3fn_x4
ADD = mybir.AluOpType.add
SUB = mybir.AluOpType.subtract
MULT = mybir.AluOpType.mult
COPY = mybir.ActivationFunctionType.Copy

P = 128
PACK = 4
HALF = S // 2
Z_PIECES = ((0, 256), (256, 384), (384, 512))


def cols16(a, b):
    return slice(a // 16, b // 16)


def tile_picked_layhopwind_none_p_kernel(tc, x_words, x_scales, w1, gn, w2, offs, n1, n2, n3, n4, out):
    nc = tc.nc
    with ExitStack() as ctx:
        keep = ctx.enter_context(tc.tile_pool(name="keep", bufs=1))
        psum = ctx.enter_context(tc.psum_pool(name="psum", bufs=1))

        def sb(name, shape, dtype, tag=""):
            return keep.tile(shape, dtype, name=name, tag=tag or name, align_bytes=64)

        lists = {}
        for name in ("offs", "n1", "n2", "n3", "n4"):
            lists[name] = sb("list_" + name, [P, S // 16], U16)

        x_bytes = sb("x_bytes", [P, T], U8)
        nc.vector.memset(x_bytes[:].bitcast(I32), 0)
        w1_rows = w1.rearrange("(p j) c -> p j c", j=PACK)
        w1_raw = [sb("w1_raw%d" % u, [P, PACK, H // 2], F32) for u in range(2)]
        nc.sync.dma_start(out=w1_raw[0][:], in_=w1_rows[:, :, 0 : H // 2])
        for q in range(4):
            nc.sync.dma_start(out=x_bytes[q:P:32, :].bitcast(I32), in_=x_scales[0, q:16:4, :].bitcast(I32))
        nc.sync.dma_start(lists["offs"][:], offs)
        nc.sync.dma_start(out=w1_raw[1][:], in_=w1_rows[:, :, H // 2 : H])
        x_table = sb("x_table", [P, T], I32)
        nc.sync.dma_start(out=x_table[:], in_=x_words[0].rearrange("p n r -> p (n r)").bitcast(I32))
        gain = sb("gain", [P, PACK], F32)
        nc.gpsimd.dma_start(out=gain[:], in_=gn.rearrange("(p t) o -> p (t o)", t=PACK))
        nc.sync.dma_start(lists["n1"][:], n1)
        nc.sync.dma_start(lists["n2"][:], n2)
        w2_raw = sb("w2_raw", [P, PACK, N], F32)
        nc.sync.dma_start(out=w2_raw[:], in_=w2.rearrange("(p j) c -> p j c", j=PACK))
        nc.sync.dma_start(lists["n3"][:], n3)
        nc.sync.dma_start(lists["n4"][:], n4)

        gain_full = sb("gain_full", [P, PACK], F32)
        gain_half = sb("gain_half", [P, PACK], F32)
        nc.gpsimd.tensor_scalar(gain_half[:], gain[:], -0.5, 0.0, MULT, ADD)
        nc.gpsimd.tensor_scalar(gain_full[:], gain[:], -1.0, 0.0, MULT, ADD)

        ident = sb("ident", [P, P], F32)
        make_identity(nc, ident[:])

        xq_scales = sb("xq_scales", [P, S], U8)
        nc.vector.tensor_copy(xq_scales[:], x_bytes[:].indirect(lists["offs"][:]))

        w1_b = sb("w1_b", [P, PACK, P, PACK], BF16)
        w1_dst = w1_b[:].rearrange("p (a b) m j -> p a m j b", b=2)
        for u in range(2):
            src = w1_raw[u][:].rearrange("p j (m a b) -> p a m j b", a=2, b=2)
            m0 = u * 64
            nc.vector.tensor_copy(w1_dst[:, 0, m0 : m0 + 64], src[:, 0])
            nc.scalar.copy(w1_dst[:, 1, m0 : m0 + 40], src[:, 1, 0:40])
            nc.vector.tensor_copy(w1_dst[:, 1, m0 + 40 : m0 + 64], src[:, 1, 40:64])
        w1_codes = sb("w1_codes", [P, H], U32)
        w1_scales = sb("w1_scales", [P, H], U8)
        for a in range(2):
            nc.vector.quantize_mx(out=w1_codes[:, a * 256 : (a + 1) * 256].bitcast(FP8X4), scales=w1_scales[:, a * 256 : (a + 1) * 256],
                                  in_=w1_b[:, 2 * a : 2 * a + 2].rearrange("p t m j -> p (t m j)"))

        xq_words = sb("xq_words", [P, S], U32)
        for u in range(2):
            a, b = u * HALF, (u + 1) * HALF
            nc.vector.tensor_copy(xq_words[:, a:b], x_table[:].bitcast(U32).indirect(lists["offs"][:, cols16(a, b)]))

        banks = [psum.tile([P, S], F32, name="bank%d" % i) for i in range(8)]

        def mm(dst, codes, scales, t, rhs, rhs_scales):
            nc.tensor.matmul_mx(out=dst, lhsT=codes[:, t * P : (t + 1) * P].bitcast(FP8X4), lhsT_scale=scales[:, t * P : (t + 1) * P],
                                rhs=rhs.bitcast(FP8X4), rhs_scale=rhs_scales, start=True, stop=True)

        half_win = [sb("half_win0", [P, S], F32)] + [sb("half_win%d" % t, [P, 2 * S], F32) for t in range(1, PACK)]
        y_last = sb("y_last", [P, S], F32)
        y_full = [half_win[t + 1][:, S:] for t in range(PACK - 1)] + [y_last[:]]
        st_win = [sb("st_win%d" % t, [P, S], F32) for t in range(PACK)]
        h_win = [sb("h_win%d" % t, [P, 2 * S], F32) for t in range(PACK - 1)] + [sb("h_win3", [P, S], F32)]
        st_last = sb("st_last", [P, S], F32)
        st_copy = [h_win[t][:, S:] for t in range(PACK - 1)] + [st_last[:]]

        for u in range(2):
            a, b = u * HALF, (u + 1) * HALF
            bank = banks[4 * u]
            mm(bank[:, 0:HALF], w1_codes, w1_scales, 0, xq_words[:, a:b], xq_scales[:, a:b])
            nc.scalar.activation(half_win[0][:, a:b], bank[:, 0:HALF], COPY, scale=gain_half[:, 0:1])
            if u == 0:
                nc.vector.tensor_scalar(y_full[0][:, a:b], bank[:, 0:HALF], gain_full[:, 0:1], None, MULT)
            else:
                nc.scalar.activation(y_full[0][:, a:b], bank[:, 0:HALF], COPY, scale=gain_full[:, 0:1])
        for t in range(1, PACK):
            mm(banks[t][:], w1_codes, w1_scales, t, xq_words[:], xq_scales[:])
        for u in range(2):
            a, b = u * HALF, (u + 1) * HALF
            nc.vector.tensor_tensor(st_win[0][:, a:b], half_win[0][:].indirect(lists["n1"][:, cols16(a, b)]), y_full[0][:, a:b], ADD)
        for t in range(1, PACK):
            nc.scalar.activation(half_win[t][:, 0:S], banks[t][:], COPY, scale=gain_half[:, t : t + 1])
            nc.scalar.activation(y_full[t], banks[t][:], COPY, scale=gain_full[:, t : t + 1])
            nc.vector.tensor_tensor(st_win[t][:], half_win[t][:].indirect(lists["n1"][:]), y_full[t], ADD)
        for t in range(PACK):
            if t < 2:
                nc.sync.dma_start(out=st_copy[t], in_=st_win[t][:])
            else:
                nc.scalar.copy(st_copy[t], st_win[t][:])

        w2_codes = sb("w2_codes", [P, N], U32)
        w2_scales = sb("w2_scales", [P, N], U8)
        w2_src = w2_raw[:].rearrange("p j (q t r i) -> p t q r j i", t=PACK, r=2, i=4)

        def w2_weave(dst, t, copy):
            copy(dst.rearrange("p (q r i) j -> p q r j i", r=2, i=4), w2_src[:, t])

        def w2_quant(src, t0, t1):
            nc.vector.quantize_mx(out=w2_codes[:, t0 * P : t1 * P].bitcast(FP8X4), scales=w2_scales[:, t0 * P : t1 * P],
                                  in_=src.rearrange("p t m j -> p (t m j)"))

        w2_early = sb("w2_early", [P, 2, P, PACK], BF16)
        w2_late = sb("w2_late", [P, 2, P, PACK], BF16)
        w2_weave(w2_early[:, 0], 0, nc.scalar.copy)
        w2_weave(w2_early[:, 1], 1, nc.scalar.copy)
        w2_weave(w2_late[:, 0], 2, nc.scalar.copy)
        w2_weave(w2_late[:, 1], 3, nc.scalar.copy)

        z_codes = sb("z_codes", [P, S], U32)
        z_scales = sb("z_scales", [P, S], U8)
        last = len(Z_PIECES) - 1
        z32 = []
        z_b = []
        for i, (a, b) in enumerate(Z_PIECES):
            z32.append(sb("z32_%d" % i, [P, PACK, b - a], F32))
            z_b.append(sb("z_b%d" % i, [P, b - a, PACK], BF16))

        def z_gather(i):
            a, b = Z_PIECES[i]
            for t in range(PACK):
                nc.vector.tensor_tensor(z32[i][:, t, :], st_win[t][:].indirect(lists["n2"][:, cols16(a, b)]), st_copy[t][:, a:b], SUB)

        def z_weave(i, copy):
            copy(z_b[i][:].rearrange("p (c i) t -> p c t i", i=4), z32[i][:].rearrange("p t (c i) -> p c t i", i=4))

        def z_quant(i):
            a, b = Z_PIECES[i]
            nc.vector.quantize_mx(out=z_codes[:, a:b].bitcast(FP8X4), scales=z_scales[:, a:b], in_=z_b[i][:].rearrange("p s t -> p (s t)"))

        def h_bank(t, i):
            return banks[0] if (t == 0 and i == last) else banks[4 + t]

        def h_mm(t, i):
            a, b = Z_PIECES[i]
            mm(h_bank(t, i)[:, a:b], w2_codes, w2_scales, t, z_codes[:, a:b], z_scales[:, a:b])

        z_gather(0)
        z_weave(0, nc.scalar.copy)
        z_gather(1)
        z_weave(1, nc.scalar.copy)
        z_gather(2)
        z_weave(2, nc.scalar.copy)
        w2_quant(w2_early[:], 0, 2)
        z_quant(0)
        z_quant(1)
        z_quant(2)
        w2_quant(w2_late[:], 2, 4)
        h_mm(0, 0)
        h_mm(0, 1)
        split = Z_PIECES[last][0]
        nc.scalar.copy(h_win[0][:, 0:split], banks[4][:, 0:split])
        h_mm(0, 2)
        h_mm(1, 0)
        h_mm(1, 1)
        nc.vector.tensor_copy(h_win[0][:, split:S], banks[0][:, split:S])
        h_mm(1, 2)
        for t in range(2, PACK):
            mm(banks[4 + t][:], w2_codes, w2_scales, t, z_codes[:], z_scales[:])
        width = {1: S, 2: HALF}
        h_pos = {t: sb("h_pos%d" % t, [P, w], F32) for t, w in width.items()}
        h_neg = {t: sb("h_neg%d" % t, [P, w], F32) for t, w in width.items()}
        for t, w in width.items():
            nc.scalar.copy(h_win[t][:, 0:S], banks[4 + t][:])
            nc.scalar.copy(h_pos[t][:], banks[4 + t][:, 0:w])
            nc.scalar.activation(h_neg[t][:], banks[4 + t][:, 0:w], COPY, scale=-1.0)
        nc.scalar.copy(h_win[3][:], banks[7][:])

        out_rows = out.rearrange("(q t r) s -> t q r s", t=PACK, r=8)
        res = [sb("res%d" % t, [P, S], F32) for t in range(PACK)]
        far = sb("far", [P, S], F32)
        nc.vector.tensor_copy(far[:], h_win[0][:].indirect(lists["n4"][:]))

        plus = {t: sb("plus%d" % t, [P, w], F32) for t, w in width.items()}
        minus = {t: sb("minus%d" % t, [P, w], F32) for t, w in width.items()}
        turned = {t: sb("turned%d" % t, [P, w], F32) for t, w in width.items()}

        def term(dst, t, name, other, first):
            w = width[t]
            nc.vector.tensor_tensor(dst[:], h_win[t][:].indirect(lists[name][:, cols16(0, w)]), other[:], MULT)
            for c in range(0, w, P):
                nc.tensor.matmul(banks[t][:, c : c + P], dst[:, c : c + P], ident[:], start=(first and c == 0), stop=(not first and c == w - P), is_transpose=True)

        def terms_plus(t):
            term(plus[t], t, "n3", h_pos[t], True)

        def terms_minus(t):
            term(minus[t], t, "n4", h_neg[t], False)
            nc.scalar.copy(turned[t][:], banks[t][:, 0 : width[t]])

        def turn_back(t):
            w = width[t]
            for c in range(0, w, P):
                nc.tensor.transpose(banks[4 + t][:, c : c + P], turned[t][:, c : c + P], ident[:])
            nc.scalar.copy(res[t][:, 0:w], banks[4 + t][:, 0:w])
            nc.sync.dma_start(out=out_rows[t][:, :, 0:w], in_=res[t][:, 0:w])

        terms_plus(1)
        terms_minus(1)
        terms_plus(2)
        terms_minus(2)
        turn_back(1)
        turn_back(2)

        def d3(dst, t, a, b, other):
            nc.vector.tensor_tensor(dst, h_win[t][:].indirect(lists["n3"][:, cols16(a, b)]), other, SUB)

        def fin(src, t, a, b):
            nc.vector.tensor_tensor(res[t][:, a:b], src, h_win[t][:, a:b], MULT)
            nc.sync.dma_start(out=out_rows[t][:, :, a:b], in_=res[t][:, a:b])

        far2 = sb("far2", [P, HALF], F32)
        far3 = sb("far3", [P, S], F32)
        diff0 = h_neg[1]
        diff2 = sb("diff2", [P, HALF], F32)
        diff3 = sb("diff3", [P, S], F32)
        d3(diff0[:], 0, 0, S, far[:])
        nc.vector.tensor_copy(far2[:], h_win[2][:].indirect(lists["n4"][:, cols16(HALF, S)]))
        fin(diff0[:], 0, 0, S)
        d3(diff2[:], 2, HALF, S, far2[:])
        nc.vector.tensor_copy(far3[:, 0:HALF], h_win[3][:].indirect(lists["n4"][:, cols16(0, HALF)]))
        fin(diff2[:], 2, HALF, S)
        nc.vector.tensor_copy(far3[:, HALF:S], h_win[3][:].indirect(lists["n4"][:, cols16(HALF, S)]))
        d3(diff3[:, 0:HALF], 3, 0, HALF, far3[:, 0:HALF])
        d3(diff3[:, HALF:384], 3, HALF, 384, far3[:, HALF:384])
        fin(diff3[:, 0:HALF], 3, 0, HALF)
        d3(diff3[:, 384:S], 3, 384, S, far3[:, 384:S])
        fin(diff3[:, HALF:384], 3, HALF, 384)
        fin(diff3[:, 384:S], 3, 384, S)
